import numpy as np, ml_dtypes
CORES = [71,199,95,223,103,231,111,239,119,247,127,255]
N = 12
import mx_ref
NC, G = 128, 2
C = np.float32(0.023)
BF = ml_dtypes.bfloat16
def tile(rs):
    return np.stack(rs, axis=2).reshape(128, -1).astype(BF)
def act(Z):
    return [np.maximum(s * z, 0) * C for z in Z for s in (1, -1)]
def pk(c, s, i=0):
    return (np.ascontiguousarray(c[:, 512 * i:512 * i + 512]), mx_ref.live(s[:, 128 * i:128 * i + 128]))
def inputs(rng, e, E):
    def f(*shape):
        v = (rng.standard_normal(shape, dtype=np.float32) * np.exp2(rng.integers(-2, 3, shape[:-1] + (1,)))).astype(BF)
        return mx_ref.spread((v.astype(np.float32) * np.exp2(rng.integers(-E, E + 1, shape[:-2] + (1, 1))).astype(np.float32)).astype(BF), rng, e)
    def packed(k):
        c = np.zeros((N, 128, k * 512), np.uint8); s = np.zeros((N, 128, k * 128), np.uint8)
        for r in range(N):
            for i in range(k):
                a, b = mx_ref.quantize(f(128, 512)); c[r][:, 512 * i:512 * i + 512] = a; s[r][:, 128 * i:128 * i + 128] = mx_ref.plane(b, rng)
        return c, s
    d = {}
    d["ac"], d["az"] = packed(1)
    d["bc"], d["bs"] = packed(1)
    d["cc"], d["cs"] = packed(1)
    d["x"] = f(N, 128, 4 * NC)
    return d
def setup_inputs(rng):
    return inputs(rng, 0, 0)
def setup_inputs_blocks(rng):
    return inputs(rng, 2, 0)
def setup_inputs_wide(rng):
    return inputs(rng, 0, 4)
def reference(ac, az, bc, bs, cc, cs, x):
    y = np.zeros((N, 128, N * NC), np.float32)
    for r in range(N):
        h = mx_ref.quantize(tile(act([mx_ref.matmul(pk(ac[i], az[i]), mx_ref.quantize(x[r])) for i in range(G)])))
        h = mx_ref.quantize(tile(act([mx_ref.matmul(pk(bc[i], bs[i]), h) for i in range(G)])))
        for j in range(N):
            y[r][:, NC * j:NC * j + NC] = mx_ref.matmul(pk(cc[j], cs[j]), h)
    return {"y": y}

@@ -1,0 +1,231 @@
+import numpy as np
+from concourse.bass import DstId, RemoteDMATransfer
+from concourse.mybir import dt, AluOpType
+
+N, G, SLOTS, PIECE, BANKS = 12, 2, 2, 160, 4
+SIM_CORES = 256
+CONST = float(np.float32(0.023))
+F8 = "float8_e4m3fn_x4"
+
+SCRATCH = {
+    "asb": ("sbuf", [128, 128], F8),
+    "asp": ("sbuf", [128, 128], "uint8"),
+    "bsb": ("sbuf", [128, 128], F8),
+    "bsp": ("sbuf", [128, 128], "uint8"),
+    "csb": ("sbuf", [128, 128 * SLOTS], F8),
+    "csp": ("sbuf", [128, 128 * SLOTS], "uint8"),
+    "ysb": ("sbuf", [128, 2 * PIECE], "float32"),
+    "psa": ("psum", [128, 1024], "float32"),
+    "psb": ("psum", [128, 1024], "float32"),
+    "psc": ("psum", [128, 512 * BANKS], "float32"),
+}
+SEMAPHORES = ["lx", "tg", "th", "sent"]
+for _k in "xgh":
+    SCRATCH["t" + _k] = ("sbuf", [128, 512], "bfloat16")
+    SCRATCH["q" + _k] = ("sbuf", [128, 128], F8)
+    SCRATCH["u" + _k] = ("sbuf", [128, 128], "uint8")
+    SEMAPHORES.append("q" + _k)
+TILES = [("a", i) for i in range(G)] + [("b", i) for i in range(G)] + [("c", j) for j in range(N)]
+for _k, _j in TILES:
+    SCRATCH["%s%dc" % (_k, _j)] = ("dram", [128, 128], F8)
+    SCRATCH["%s%dp" % (_k, _j)] = ("dram", [128, 128], "uint8")
+    SEMAPHORES += ["r_%s%dc" % (_k, _j), "r_%s%dp" % (_k, _j), "s_%s%d" % (_k, _j), "m_%s%d" % (_k, _j)]
+SEMAPHORES += ["lac", "lap", "lbc", "lbp", "lcc", "lcp"]
+PIECES = [(a, min(a + PIECE, 128 * N)) for a in range(0, 128 * N, PIECE)]
+SEMAPHORES += ["cp%d" % i for i in range(len(PIECES))] + ["st%d" % i for i in range(len(PIECES))]
+
+
+def plan(T, topo):
+    todo = {}
+
+    def send(src, layer, j, dsts, mask, relayed):
+        if dsts:
+            todo.setdefault(src, []).append((layer, j, dsts, mask, relayed))
+
+    def both(src, dsts):
+        m = topo.mask(src, dsts[0]) if dsts else 0
+        for d in dsts:
+            m &= topo.mask(src, d)
+        return m
+
+    for j in range(N):
+        s = T.cores[j]
+        same = [d for d in T.cores if d != s and topo.same_plane(s, d)]
+        rest = [d for d in T.cores if d != s and not topo.same_plane(s, d)]
+        if j < G:
+            halves = [same, rest] if j == 0 else [rest, same]
+            off = both(s, same + rest)
+            here = [c for c in range(SIM_CORES) if c != s and topo.host(c) == topo.host(s) and topo.chip(c) == topo.chip(s)]
+            for layer, near, half in (("b", False, halves[0]), ("c", True, halves[1])):
+                send(s, "a", j, half, off, False)
+                cand = [c for c in here if (topo.die(c) == topo.die(s)) == near]
+                to_rest = [c for c in cand if all(topo.may_write(c, d) for d in rest)][-1]
+                to_same = [c for c in cand if c != to_rest][-1]
+                hand = [to_rest, to_same]
+                send(s, layer, j, hand, both(s, hand) & ~off, False)
+                send(to_rest, layer, j, rest, both(to_rest, rest), True)
+                send(to_same, layer, j, same, both(to_same, same), True)
+        else:
+            mate = [d for d in rest if topo.mates(s, d)]
+            far = [d for d in rest if not topo.mates(s, d)]
+            relay = [c for c in range(SIM_CORES) if topo.mates(s, c) and topo.die(c) != topo.die(s)][-1]
+            first = [relay] + mate + same
+            send(s, "c", j, first, both(s, first), False)
+            send(relay, "c", j, far, both(relay, far), True)
+    return todo
+
+
+def count(mask):
+    return bin(mask).count("1")
+
+
+def copies(k):
+    a, b = PIECES[k]
+    return (b - 1) // 128 - a // 128 + 1
+
+
+def runs(k, base):
+    a, b = PIECES[k]
+    turn = 128 * (N - base)
+    cut = [a] + ([turn] if a < turn < b else []) + [b]
+    return [(lo, hi, (128 * base + lo) % (128 * N)) for lo, hi in zip(cut, cut[1:])]
+
+
+def piece_of(pos):
+    return [k for k, (a, b) in enumerate(PIECES) if a <= pos < b][0]
+
+
+def rank_program(g, core, T, topo):
+    rank = T.rank_of(core)
+    todo = plan(T, topo)
+    mine = todo.get(core, [])
+    if rank is None and not mine:
+        return
+    u8 = dt.uint8
+
+    came = {}
+    for src in todo:
+        for layer, j, dsts, mask, relayed in todo[src]:
+            if core in dsts:
+                came[(layer, j)] = count(mask)
+
+    def codes(layer, j):
+        return T["%s%dc" % (layer, j)][:].bitcast(u8)
+
+    def plane(layer, j):
+        return T["%s%dp" % (layer, j)][:]
+
+    total, loaded = 0, set()
+    for layer, j, dsts, mask, relayed in mine:
+        for part, view in (("c", codes), ("p", plane)):
+            name = "r_%s%d%s" % (layer, j, part)
+            if relayed:
+                g.wait_ge(T.sem[name], came[(layer, j)])
+            elif (layer, part) not in loaded:
+                g.wait_ge(T.sem["l%s%s" % (layer, part)], 16)
+                loaded.add((layer, part))
+            ids = []
+            for d in dsts:
+                rid, pid = topo.addr(d, core)
+                ids.append(DstId(rid=rid, pnc=pid))
+            g.remote_dma_fused([RemoteDMATransfer(dst_ids=ids, dma_engine_mask=mask, remote_sem=T.sem[name],
+                                                  srcs=[view(layer, j)], dsts=[view(layer, j) for d in dsts])],
+                               local_sem=T.sem.sent)
+            total += count(mask)
+    if rank is None:
+        g.wait_ge(T.sem.sent, total)
+        return
+
+    sync, scal, vec, ten = g.sync, g.scalar, g.vector, g.tensor
+    CODES = {"a": T.ac, "b": T.bc, "c": T.cc}
+    PLANE = {"a": T.az, "b": T.bs, "c": T.cs}
+    SB = {"a": T.asb, "b": T.bsb, "c": T.csb}
+    SP = {"a": T.asp, "b": T.bsp, "c": T.csp}
+
+    ab = sorted(range(G), key=lambda i: (i != rank, topo.same_plane(core, T.cores[i]) != (i == 0)))
+    base = 2 * (rank // 2)
+    order = [(base + n) % N for n in range(N)]
+
+    def fetch(queue, layer, j, slot, part):
+        if j != rank:
+            queue.wait_ge(T.sem["r_%s%d%s" % (layer, j, part)], came[(layer, j)])
+        a, b = 128 * slot, 128 * slot + 128
+        if part == "c":
+            out, src = SB[layer][:, a:b].bitcast(u8), CODES[layer][:] if j == rank else codes(layer, j)
+        else:
+            out, src = SP[layer][:, a:b], PLANE[layer][:] if j == rank else plane(layer, j)
+        queue.dma_start(out, src).then_inc(T.sem["s_%s%d" % (layer, j)], 16)
+
+    for layer in (["a", "b", "c"] if rank < G else ["c"]):
+        sync.dma_start(codes(layer, rank), CODES[layer][:]).then_inc(T.sem["l%sc" % layer], 16)
+        scal.dma_start(plane(layer, rank), PLANE[layer][:]).then_inc(T.sem["l%sp" % layer], 16)
+    scal.dma_start(T.tx[:], T.x[:]).then_inc(T.sem.lx, 16)
+
+    for n in range(SLOTS):
+        if order[n] == rank:
+            fetch(sync, "c", rank, n, "c")
+            fetch(sync, "c", rank, n, "p")
+    for k, i in enumerate(ab):
+        for queue, part in ((sync, "c"), (scal, "p")):
+            if k:
+                queue.wait_ge(T.sem["m_a%d" % ab[0]], 1)
+            fetch(queue, "a", i, 0, part)
+    fetch(sync, "b", ab[0], 0, "c")
+    fetch(sync, "b", ab[0], 0, "p")
+    scal.wait_ge(T.sem["m_b%d" % ab[0]], 1)
+    fetch(scal, "b", ab[1], 0, "c")
+    fetch(scal, "b", ab[1], 0, "p")
+    for n in range(N):
+        if n < SLOTS and order[n] == rank:
+            continue
+        if n >= SLOTS:
+            sync.wait_ge(T.sem["m_c%d" % order[n - SLOTS]], 1)
+        fetch(sync, "c", order[n], n % SLOTS, "c")
+        fetch(sync, "c", order[n], n % SLOTS, "p")
+
+    vec.wait_ge(T.sem.lx, 16)
+    vec.quantize_mx(T.qx[:], T.ux[:], T.tx[:]).then_inc(T.sem.qx, 1)
+    for layer, to, ps in (("a", "g", T.psa), ("b", "h", T.psb)):
+        tile = T["t" + to]
+        for i in ab:
+            vec.wait_ge(T.sem["m_%s%d" % (layer, i)], 1)
+            z = ps[:, 512 * i:512 * i + 128]
+            for k, c in ((0, CONST), (1, -CONST)):
+                vec.tensor_scalar(tile[:, 2 * i + k:512:4], z, c, 0.0, AluOpType.mult, AluOpType.max).then_inc(T.sem["t" + to], 1)
+        vec.wait_ge(T.sem["t" + to], 2 * G)
+        vec.quantize_mx(T["q" + to][:], T["u" + to][:], tile[:]).then_inc(T.sem["q" + to], 1)
+
+    for layer, of, ps in (("a", "x", T.psa), ("b", "g", T.psb)):
+        ten.wait_ge(T.sem["q" + of], 1)
+        for i in ab:
+            ten.wait_ge(T.sem["s_%s%d" % (layer, i)], 32)
+            ten.matmul_mx(ps[:, 512 * i:512 * i + 128], SB[layer][:], SP[layer][:],
+                          T["q" + of][:], T["u" + of][:], True, True).then_inc(T.sem["m_%s%d" % (layer, i)], 1)
+    ten.wait_ge(T.sem.qh, 1)
+    for n in range(N):
+        j, a, bank = order[n], 128 * (n % SLOTS), n % BANKS
+        ten.wait_ge(T.sem["s_c%d" % j], 32)
+        if n >= BANKS:
+            k = piece_of(128 * (n - BANKS) + 127)
+            ten.wait_ge(T.sem["cp%d" % k], copies(k))
+        ten.matmul_mx(T.psc[:, 512 * bank:512 * bank + 128], T.csb[:, a:a + 128], T.csp[:, a:a + 128],
+                      T.qh[:], T.uh[:], True, True).then_inc(T.sem["m_c%d" % j], 1)
+
+    seen = set()
+    for k, (a, b) in enumerate(PIECES):
+        off = PIECE * (k % 2) - a
+        if k >= 2:
+            vec.wait_ge(T.sem["st%d" % (k - 2)], 16 * len(runs(k - 2, base)))
+        for n in range(a // 128, (b - 1) // 128 + 1):
+            lo, hi = max(a, 128 * n), min(b, 128 * n + 128)
+            if n not in seen:
+                vec.wait_ge(T.sem["m_c%d" % order[n]], 1)
+                seen.add(n)
+            col = 512 * (n % BANKS) - 128 * n
+            vec.tensor_copy(T.ysb[:, off + lo:off + hi], T.psc[:, col + lo:col + hi]).then_inc(T.sem["cp%d" % k], 1)
+        scal.wait_ge(T.sem["cp%d" % k], copies(k))
+        for lo, hi, y in runs(k, base):
+            scal.dma_start(T.y[:, y:y + hi - lo], T.ysb[:, off + lo:off + hi]).then_inc(T.sem["st%d" % k], 16)
+    for k in range(len(PIECES) - 2, len(PIECES)):
+        scal.wait_ge(T.sem["st%d" % k], 16 * len(runs(k, base)))
+    g.wait_ge(T.sem.sent, total)

@@ -2,7 +2,7 @@ import numpy as np
 from concourse.bass import DstId, RemoteDMATransfer
 from concourse.mybir import dt, AluOpType
 
-N, G, SLOTS, PIECE, BANKS = 12, 2, 2, 160, 4
+N, G, SLOTS, PLANES, STAGE, BANKS = 12, 2, 2, 4, 2, 4
 SIM_CORES = 256
 CONST = float(np.float32(0.023))
 F8 = "float8_e4m3fn_x4"
@@ -13,8 +13,8 @@ SCRATCH = {
     "bsb": ("sbuf", [128, 128], F8),
     "bsp": ("sbuf", [128, 128], "uint8"),
     "csb": ("sbuf", [128, 128 * SLOTS], F8),
-    "csp": ("sbuf", [128, 128 * SLOTS], "uint8"),
-    "ysb": ("sbuf", [128, 2 * PIECE], "float32"),
+    "csp": ("sbuf", [128, 128 * PLANES], "uint8"),
+    "ysb": ("sbuf", [128, 128 * STAGE], "float32"),
     "psa": ("psum", [128, 1024], "float32"),
     "psb": ("psum", [128, 1024], "float32"),
     "psc": ("psum", [128, 512 * BANKS], "float32"),
@@ -31,16 +31,19 @@ for _k, _j in TILES:
     SCRATCH["%s%dp" % (_k, _j)] = ("dram", [128, 128], "uint8")
     SEMAPHORES += ["r_%s%dc" % (_k, _j), "r_%s%dp" % (_k, _j), "s_%s%d" % (_k, _j), "m_%s%d" % (_k, _j)]
 SEMAPHORES += ["lac", "lap", "lbc", "lbp", "lcc", "lcp"]
-PIECES = [(a, min(a + PIECE, 128 * N)) for a in range(0, 128 * N, PIECE)]
-SEMAPHORES += ["cp%d" % i for i in range(len(PIECES))] + ["st%d" % i for i in range(len(PIECES))]
+SEMAPHORES += ["cp%d" % i for i in range(N)] + ["st%d" % i for i in range(N)]
+
+
+def first_half(T, topo, s, d):
+    return topo.same_plane(s, d) == (topo.host(s) == topo.host(d))
+
+
+def has_mate(T, topo, c):
+    return any(topo.mates(c, e) for e in T.cores)
 
 
 def plan(T, topo):
-    todo = {}
-
-    def send(src, layer, j, dsts, mask, relayed):
-        if dsts:
-            todo.setdefault(src, []).append((layer, j, dsts, mask, relayed))
+    todo, later = {}, []
 
     def both(src, dsts):
         m = topo.mask(src, dsts[0]) if dsts else 0
@@ -48,51 +51,52 @@ def plan(T, topo):
             m &= topo.mask(src, d)
         return m
 
+    def send(src, layer, j, dsts, relayed, leave_free=0):
+        if dsts:
+            todo.setdefault(src, []).append((layer, j, dsts, both(src, dsts) & ~leave_free, relayed))
+
     for j in range(N):
         s = T.cores[j]
         same = [d for d in T.cores if d != s and topo.same_plane(s, d)]
         rest = [d for d in T.cores if d != s and not topo.same_plane(s, d)]
+        over = [c for c in range(SIM_CORES) if topo.host(c) == topo.host(s) and topo.chip(c) == topo.chip(s)
+                and topo.die(c) != topo.die(s)]
         if j < G:
-            halves = [same, rest] if j == 0 else [rest, same]
-            off = both(s, same + rest)
-            here = [c for c in range(SIM_CORES) if c != s and topo.host(c) == topo.host(s) and topo.chip(c) == topo.chip(s)]
-            for layer, near, half in (("b", False, halves[0]), ("c", True, halves[1])):
-                send(s, "a", j, half, off, False)
-                cand = [c for c in here if (topo.die(c) == topo.die(s)) == near]
-                to_rest = [c for c in cand if all(topo.may_write(c, d) for d in rest)][-1]
-                to_same = [c for c in cand if c != to_rest][-1]
-                hand = [to_rest, to_same]
-                send(s, layer, j, hand, both(s, hand) & ~off, False)
-                send(to_rest, layer, j, rest, both(to_rest, rest), True)
-                send(to_same, layer, j, same, both(to_same, same), True)
+            other = T.cores[1 - j]
+            mated = [d for d in rest + same if has_mate(T, topo, d) and first_half(T, topo, s, d)]
+            swap = [(d, e) for d in mated for e in T.cores if topo.mates(d, e)]
+            lone = [d for d in rest if not has_mate(T, topo, d)]
+            on = list(zip(mated, lone))
+            send(s, "a", j, mated, False)
+            if j == 0:
+                send(s, "a", j, lone, False)
+                send(s, "b", j, mated, False)
+                later += [("a", j, d, e) for d, e in swap + [(mated[2], other)]]
+                later += [("b", j, d, e) for d, e in swap + on + [(mated[3], other)]]
+            else:
+                send(s, "b", j, lone + mated, False)
+                later += [("a", j, d, e) for d, e in on + swap + [(mated[2], other)]]
+                later += [("b", j, d, e) for d, e in [(lone[0], other)] + swap]
+            to_rest = [c for c in over if all(topo.may_write(c, d) for d in rest)][0]
+            to_same = [c for c in over if c != to_rest][0]
+            send(s, "c", j, [to_same, to_rest], False, both(s, same + rest))
+            send(to_rest, "c", j, rest, True)
         else:
             mate = [d for d in rest if topo.mates(s, d)]
-            far = [d for d in rest if not topo.mates(s, d)]
-            relay = [c for c in range(SIM_CORES) if topo.mates(s, c) and topo.die(c) != topo.die(s)][-1]
-            first = [relay] + mate + same
-            send(s, "c", j, first, both(s, first), False)
-            send(relay, "c", j, far, both(relay, far), True)
+            to_rest = [c for c in range(SIM_CORES) if topo.mates(s, c) and topo.die(c) != topo.die(s)][-1]
+            to_same = over[0]
+            send(s, "c", j, [to_same, to_rest] + mate, False)
+            send(to_rest, "c", j, [d for d in rest if d not in mate], True)
+        send(to_same, "c", j, same, True)
+    for which in "ab":
+        for layer, j, d, e in later:
+            if layer == which:
+                send(d, layer, j, [e], True)
     return todo
 
 
 def count(mask):
     return bin(mask).count("1")
-
-
-def copies(k):
-    a, b = PIECES[k]
-    return (b - 1) // 128 - a // 128 + 1
-
-
-def runs(k, base):
-    a, b = PIECES[k]
-    turn = 128 * (N - base)
-    cut = [a] + ([turn] if a < turn < b else []) + [b]
-    return [(lo, hi, (128 * base + lo) % (128 * N)) for lo, hi in zip(cut, cut[1:])]
-
-
-def piece_of(pos):
-    return [k for k, (a, b) in enumerate(PIECES) if a <= pos < b][0]
 
 
 def rank_program(g, core, T, topo):
@@ -142,9 +146,20 @@ def rank_program(g, core, T, topo):
     SB = {"a": T.asb, "b": T.bsb, "c": T.csb}
     SP = {"a": T.asp, "b": T.bsp, "c": T.csp}
 
-    ab = sorted(range(G), key=lambda i: (i != rank, topo.same_plane(core, T.cores[i]) != (i == 0)))
+    if rank < G:
+        first = {"a": rank, "b": rank}
+    elif has_mate(T, topo, core):
+        k = [i for i in range(G) if first_half(T, topo, T.cores[i], core)][0]
+        first = {"a": k, "b": k}
+    else:
+        first = {"a": 0, "b": 1}
+    ab = {layer: [first[layer], 1 - first[layer]] for layer in "ab"}
     base = 2 * (rank // 2)
-    order = [(base + n) % N for n in range(N)]
+
+    def late(j):
+        d = T.cores[j]
+        return 0 if d == core else 4 if j < G else 1 if topo.same_plane(core, d) else 2 if topo.mates(core, d) else 3
+    order = sorted(range(N), key=lambda j: (late(j), (j - base) % N))
 
     def fetch(queue, layer, j, slot, part):
         if j != rank:
@@ -161,33 +176,32 @@ def rank_program(g, core, T, topo):
         scal.dma_start(plane(layer, rank), PLANE[layer][:]).then_inc(T.sem["l%sp" % layer], 16)
     scal.dma_start(T.tx[:], T.x[:]).then_inc(T.sem.lx, 16)
 
-    for n in range(SLOTS):
-        if order[n] == rank:
-            fetch(sync, "c", rank, n, "c")
-            fetch(sync, "c", rank, n, "p")
-    for k, i in enumerate(ab):
-        for queue, part in ((sync, "c"), (scal, "p")):
-            if k:
-                queue.wait_ge(T.sem["m_a%d" % ab[0]], 1)
-            fetch(queue, "a", i, 0, part)
-    fetch(sync, "b", ab[0], 0, "c")
-    fetch(sync, "b", ab[0], 0, "p")
-    scal.wait_ge(T.sem["m_b%d" % ab[0]], 1)
-    fetch(scal, "b", ab[1], 0, "c")
-    fetch(scal, "b", ab[1], 0, "p")
-    for n in range(N):
-        if n < SLOTS and order[n] == rank:
-            continue
-        if n >= SLOTS:
-            sync.wait_ge(T.sem["m_c%d" % order[n - SLOTS]], 1)
-        fetch(sync, "c", order[n], n % SLOTS, "c")
-        fetch(sync, "c", order[n], n % SLOTS, "p")
+    def refill(queue, n, part):
+        depth = SLOTS if part == "c" else PLANES
+        if n >= depth:
+            queue.wait_ge(T.sem["m_c%d" % order[n - depth]], 1)
+        fetch(queue, "c", order[n], n % depth, part)
+    refill(sync, 0, "c")
+    refill(sync, 0, "p")
+    fetch(sync, "a", ab["a"][0], 0, "c")
+    fetch(scal, "a", ab["a"][0], 0, "p")
+    fetch(sync, "b", ab["b"][0], 0, "c")
+    fetch(sync, "b", ab["b"][0], 0, "p")
+    for layer in "ab":
+        scal.wait_ge(T.sem["m_%s%d" % (layer, ab[layer][0])], 1)
+        fetch(scal, layer, ab[layer][1], 0, "c")
+        fetch(scal, layer, ab[layer][1], 0, "p")
+    for n in range(1, PLANES):
+        for part in ("cp" if n < SLOTS else "p"):
+            refill(sync, n, part)
+    for n in range(SLOTS, N):
+        refill(sync, n, "c")
 
     vec.wait_ge(T.sem.lx, 16)
     vec.quantize_mx(T.qx[:], T.ux[:], T.tx[:]).then_inc(T.sem.qx, 1)
     for layer, to, ps in (("a", "g", T.psa), ("b", "h", T.psb)):
         tile = T["t" + to]
-        for i in ab:
+        for i in ab[layer]:
             vec.wait_ge(T.sem["m_%s%d" % (layer, i)], 1)
             z = ps[:, 512 * i:512 * i + 128]
             for k, c in ((0, CONST), (1, -CONST)):
@@ -197,35 +211,29 @@ def rank_program(g, core, T, topo):
 
     for layer, of, ps in (("a", "x", T.psa), ("b", "g", T.psb)):
         ten.wait_ge(T.sem["q" + of], 1)
-        for i in ab:
+        for i in ab[layer]:
             ten.wait_ge(T.sem["s_%s%d" % (layer, i)], 32)
             ten.matmul_mx(ps[:, 512 * i:512 * i + 128], SB[layer][:], SP[layer][:],
                           T["q" + of][:], T["u" + of][:], True, True).then_inc(T.sem["m_%s%d" % (layer, i)], 1)
     ten.wait_ge(T.sem.qh, 1)
     for n in range(N):
-        j, a, bank = order[n], 128 * (n % SLOTS), n % BANKS
+        j, a, p, bank = order[n], 128 * (n % SLOTS), 128 * (n % PLANES), 512 * (n % BANKS)
         ten.wait_ge(T.sem["s_c%d" % j], 32)
         if n >= BANKS:
-            k = piece_of(128 * (n - BANKS) + 127)
-            ten.wait_ge(T.sem["cp%d" % k], copies(k))
-        ten.matmul_mx(T.psc[:, 512 * bank:512 * bank + 128], T.csb[:, a:a + 128], T.csp[:, a:a + 128],
+            ten.wait_ge(T.sem["cp%d" % (n - BANKS)], 1)
+        ten.matmul_mx(T.psc[:, bank:bank + 128], T.csb[:, a:a + 128], T.csp[:, p:p + 128],
                       T.qh[:], T.uh[:], True, True).then_inc(T.sem["m_c%d" % j], 1)
 
-    seen = set()
-    for k, (a, b) in enumerate(PIECES):
-        off = PIECE * (k % 2) - a
-        if k >= 2:
-            vec.wait_ge(T.sem["st%d" % (k - 2)], 16 * len(runs(k - 2, base)))
-        for n in range(a // 128, (b - 1) // 128 + 1):
-            lo, hi = max(a, 128 * n), min(b, 128 * n + 128)
-            if n not in seen:
-                vec.wait_ge(T.sem["m_c%d" % order[n]], 1)
-                seen.add(n)
-            col = 512 * (n % BANKS) - 128 * n
-            vec.tensor_copy(T.ysb[:, off + lo:off + hi], T.psc[:, col + lo:col + hi]).then_inc(T.sem["cp%d" % k], 1)
-        scal.wait_ge(T.sem["cp%d" % k], copies(k))
-        for lo, hi, y in runs(k, base):
-            scal.dma_start(T.y[:, y:y + hi - lo], T.ysb[:, off + lo:off + hi]).then_inc(T.sem["st%d" % k], 16)
-    for k in range(len(PIECES) - 2, len(PIECES)):
-        scal.wait_ge(T.sem["st%d" % k], 16 * len(runs(k, base)))
+    for n in range(N):
+        j, a, bank = order[n], 128 * (n % STAGE), 512 * (n % BANKS)
+        if n >= STAGE:
+            vec.wait_ge(T.sem["st%d" % (n - STAGE)], 16)
+        vec.wait_ge(T.sem["m_c%d" % j], 1)
+        vec.tensor_copy(T.ysb[:, a:a + 128], T.psc[:, bank:bank + 128]).then_inc(T.sem["cp%d" % n], 1)
+        scal.wait_ge(T.sem["cp%d" % n], 1)
+        scal.dma_start(T.y[:, 128 * j:128 * j + 128], T.ysb[:, a:a + 128]).then_inc(T.sem["st%d" % n], 16)
+        if n + PLANES < N:
+            refill(scal, n + PLANES, "p")
+    for n in range(N - STAGE, N):
+        scal.wait_ge(T.sem["st%d" % n], 16)
     g.wait_ge(T.sem.sent, total)

import numpy as np
from concourse.bass import DstId, RemoteDMATransfer
from concourse.mybir import dt, AluOpType

N, G, SLOTS, PLANES, STAGE, BANKS = 12, 2, 2, 4, 2, 4
SIM_CORES = 256
CONST = float(np.float32(0.023))
F8 = "float8_e4m3fn_x4"

SCRATCH = {
    "asb": ("sbuf", [128, 128], F8),
    "asp": ("sbuf", [128, 128], "uint8"),
    "bsb": ("sbuf", [128, 128], F8),
    "bsp": ("sbuf", [128, 128], "uint8"),
    "csb": ("sbuf", [128, 128 * SLOTS], F8),
    "csp": ("sbuf", [128, 128 * PLANES], "uint8"),
    "ysb": ("sbuf", [128, 128 * STAGE], "float32"),
    "psa": ("psum", [128, 1024], "float32"),
    "psb": ("psum", [128, 1024], "float32"),
    "psc": ("psum", [128, 512 * BANKS], "float32"),
}
SEMAPHORES = ["lx", "tg", "th", "sent"]
for _k in "xgh":
    SCRATCH["t" + _k] = ("sbuf", [128, 512], "bfloat16")
    SCRATCH["q" + _k] = ("sbuf", [128, 128], F8)
    SCRATCH["u" + _k] = ("sbuf", [128, 128], "uint8")
    SEMAPHORES.append("q" + _k)
TILES = [("a", i) for i in range(G)] + [("b", i) for i in range(G)] + [("c", j) for j in range(N)]
for _k, _j in TILES:
    SCRATCH["%s%dc" % (_k, _j)] = ("dram", [128, 128], F8)
    SCRATCH["%s%dp" % (_k, _j)] = ("dram", [128, 128], "uint8")
    SEMAPHORES += ["r_%s%dc" % (_k, _j), "r_%s%dp" % (_k, _j), "s_%s%d" % (_k, _j), "m_%s%d" % (_k, _j)]
SEMAPHORES += ["lac", "lap", "lbc", "lbp", "lcc", "lcp"]
SEMAPHORES += ["cp%d" % i for i in range(N)] + ["st%d" % i for i in range(N)]


def first_half(T, topo, s, d):
    return topo.same_plane(s, d) == (topo.host(s) == topo.host(d))


def has_mate(T, topo, c):
    return any(topo.mates(c, e) for e in T.cores)


def plan(T, topo):
    todo, later = {}, []

    def both(src, dsts):
        m = topo.mask(src, dsts[0]) if dsts else 0
        for d in dsts:
            m &= topo.mask(src, d)
        return m

    def send(src, layer, j, dsts, relayed, leave_free=0):
        if dsts:
            todo.setdefault(src, []).append((layer, j, dsts, both(src, dsts) & ~leave_free, relayed))

    for j in range(N):
        s = T.cores[j]
        same = [d for d in T.cores if d != s and topo.same_plane(s, d)]
        rest = [d for d in T.cores if d != s and not topo.same_plane(s, d)]
        over = [c for c in range(SIM_CORES) if topo.host(c) == topo.host(s) and topo.chip(c) == topo.chip(s)
                and topo.die(c) != topo.die(s)]
        if j < G:
            other = T.cores[1 - j]
            mated = [d for d in rest + same if has_mate(T, topo, d) and first_half(T, topo, s, d)]
            swap = [(d, e) for d in mated for e in T.cores if topo.mates(d, e)]
            lone = [d for d in rest if not has_mate(T, topo, d)]
            on = list(zip(mated, lone))
            send(s, "a", j, mated, False)
            if j == 0:
                send(s, "a", j, lone, False)
                send(s, "b", j, mated, False)
                later += [("a", j, d, e) for d, e in swap + [(mated[2], other)]]
                later += [("b", j, d, e) for d, e in swap + on + [(mated[3], other)]]
            else:
                send(s, "b", j, lone + mated, False)
                later += [("a", j, d, e) for d, e in on + swap + [(mated[2], other)]]
                later += [("b", j, d, e) for d, e in [(lone[0], other)] + swap]
            to_rest = [c for c in over if all(topo.may_write(c, d) for d in rest)][0]
            to_same = [c for c in over if c != to_rest][0]
            send(s, "c", j, [to_same, to_rest], False, both(s, same + rest))
            send(to_rest, "c", j, rest, True)
        else:
            mate = [d for d in rest if topo.mates(s, d)]
            to_rest = [c for c in range(SIM_CORES) if topo.mates(s, c) and topo.die(c) != topo.die(s)][-1]
            to_same = over[0]
            send(s, "c", j, [to_same, to_rest] + mate, False)
            send(to_rest, "c", j, [d for d in rest if d not in mate], True)
        send(to_same, "c", j, same, True)
    for which in "ab":
        for layer, j, d, e in later:
            if layer == which:
                send(d, layer, j, [e], True)
    return todo


def count(mask):
    return bin(mask).count("1")


def rank_program(g, core, T, topo):
    rank = T.rank_of(core)
    todo = plan(T, topo)
    mine = todo.get(core, [])
    if rank is None and not mine:
        return
    u8 = dt.uint8

    came = {}
    for src in todo:
        for layer, j, dsts, mask, relayed in todo[src]:
            if core in dsts:
                came[(layer, j)] = count(mask)

    def codes(layer, j):
        return T["%s%dc" % (layer, j)][:].bitcast(u8)

    def plane(layer, j):
        return T["%s%dp" % (layer, j)][:]

    total, loaded = 0, set()
    for layer, j, dsts, mask, relayed in mine:
        for part, view in (("c", codes), ("p", plane)):
            name = "r_%s%d%s" % (layer, j, part)
            if relayed:
                g.wait_ge(T.sem[name], came[(layer, j)])
            elif (layer, part) not in loaded:
                g.wait_ge(T.sem["l%s%s" % (layer, part)], 16)
                loaded.add((layer, part))
            ids = []
            for d in dsts:
                rid, pid = topo.addr(d, core)
                ids.append(DstId(rid=rid, pnc=pid))
            g.remote_dma_fused([RemoteDMATransfer(dst_ids=ids, dma_engine_mask=mask, remote_sem=T.sem[name],
                                                  srcs=[view(layer, j)], dsts=[view(layer, j) for d in dsts])],
                               local_sem=T.sem.sent)
            total += count(mask)
    if rank is None:
        g.wait_ge(T.sem.sent, total)
        return

    sync, scal, vec, ten = g.sync, g.scalar, g.vector, g.tensor
    CODES = {"a": T.ac, "b": T.bc, "c": T.cc}
    PLANE = {"a": T.az, "b": T.bs, "c": T.cs}
    SB = {"a": T.asb, "b": T.bsb, "c": T.csb}
    SP = {"a": T.asp, "b": T.bsp, "c": T.csp}

    if rank < G:
        first = {"a": rank, "b": rank}
    elif has_mate(T, topo, core):
        k = [i for i in range(G) if first_half(T, topo, T.cores[i], core)][0]
        first = {"a": k, "b": k}
    else:
        first = {"a": 0, "b": 1}
    ab = {layer: [first[layer], 1 - first[layer]] for layer in "ab"}
    base = 2 * (rank // 2)

    def late(j):
        d = T.cores[j]
        return 0 if d == core else 4 if j < G else 1 if topo.same_plane(core, d) else 2 if topo.mates(core, d) else 3
    order = sorted(range(N), key=lambda j: (late(j), (j - base) % N))

    def fetch(queue, layer, j, slot, part):
        if j != rank:
            queue.wait_ge(T.sem["r_%s%d%s" % (layer, j, part)], came[(layer, j)])
        a, b = 128 * slot, 128 * slot + 128
        if part == "c":
            out, src = SB[layer][:, a:b].bitcast(u8), CODES[layer][:] if j == rank else codes(layer, j)
        else:
            out, src = SP[layer][:, a:b], PLANE[layer][:] if j == rank else plane(layer, j)
        queue.dma_start(out, src).then_inc(T.sem["s_%s%d" % (layer, j)], 16)

    for layer in (["a", "b", "c"] if rank < G else ["c"]):
        sync.dma_start(codes(layer, rank), CODES[layer][:]).then_inc(T.sem["l%sc" % layer], 16)
        scal.dma_start(plane(layer, rank), PLANE[layer][:]).then_inc(T.sem["l%sp" % layer], 16)
    scal.dma_start(T.tx[:], T.x[:]).then_inc(T.sem.lx, 16)

    def refill(queue, n, part):
        depth = SLOTS if part == "c" else PLANES
        if n >= depth:
            queue.wait_ge(T.sem["m_c%d" % order[n - depth]], 1)
        fetch(queue, "c", order[n], n % depth, part)
    refill(sync, 0, "c")
    refill(sync, 0, "p")
    fetch(sync, "a", ab["a"][0], 0, "c")
    fetch(scal, "a", ab["a"][0], 0, "p")
    fetch(sync, "b", ab["b"][0], 0, "c")
    fetch(sync, "b", ab["b"][0], 0, "p")
    for layer in "ab":
        scal.wait_ge(T.sem["m_%s%d" % (layer, ab[layer][0])], 1)
        fetch(scal, layer, ab[layer][1], 0, "c")
        fetch(scal, layer, ab[layer][1], 0, "p")
    for n in range(1, PLANES):
        for part in ("cp" if n < SLOTS else "p"):
            refill(sync, n, part)
    for n in range(SLOTS, N):
        refill(sync, n, "c")

    vec.wait_ge(T.sem.lx, 16)
    vec.quantize_mx(T.qx[:], T.ux[:], T.tx[:]).then_inc(T.sem.qx, 1)
    for layer, to, ps in (("a", "g", T.psa), ("b", "h", T.psb)):
        tile = T["t" + to]
        for i in ab[layer]:
            vec.wait_ge(T.sem["m_%s%d" % (layer, i)], 1)
            z = ps[:, 512 * i:512 * i + 128]
            for k, c in ((0, CONST), (1, -CONST)):
                vec.tensor_scalar(tile[:, 2 * i + k:512:4], z, c, 0.0, AluOpType.mult, AluOpType.max).then_inc(T.sem["t" + to], 1)
        vec.wait_ge(T.sem["t" + to], 2 * G)
        vec.quantize_mx(T["q" + to][:], T["u" + to][:], tile[:]).then_inc(T.sem["q" + to], 1)

    for layer, of, ps in (("a", "x", T.psa), ("b", "g", T.psb)):
        ten.wait_ge(T.sem["q" + of], 1)
        for i in ab[layer]:
            ten.wait_ge(T.sem["s_%s%d" % (layer, i)], 32)
            ten.matmul_mx(ps[:, 512 * i:512 * i + 128], SB[layer][:], SP[layer][:],
                          T["q" + of][:], T["u" + of][:], True, True).then_inc(T.sem["m_%s%d" % (layer, i)], 1)
    ten.wait_ge(T.sem.qh, 1)
    for n in range(N):
        j, a, p, bank = order[n], 128 * (n % SLOTS), 128 * (n % PLANES), 512 * (n % BANKS)
        ten.wait_ge(T.sem["s_c%d" % j], 32)
        if n >= BANKS:
            ten.wait_ge(T.sem["cp%d" % (n - BANKS)], 1)
        ten.matmul_mx(T.psc[:, bank:bank + 128], T.csb[:, a:a + 128], T.csp[:, p:p + 128],
                      T.qh[:], T.uh[:], True, True).then_inc(T.sem["m_c%d" % j], 1)

    for n in range(N):
        j, a, bank = order[n], 128 * (n % STAGE), 512 * (n % BANKS)
        if n >= STAGE:
            vec.wait_ge(T.sem["st%d" % (n - STAGE)], 16)
        vec.wait_ge(T.sem["m_c%d" % j], 1)
        vec.tensor_copy(T.ysb[:, a:a + 128], T.psc[:, bank:bank + 128]).then_inc(T.sem["cp%d" % n], 1)
        scal.wait_ge(T.sem["cp%d" % n], 1)
        scal.dma_start(T.y[:, 128 * j:128 * j + 128], T.ysb[:, a:a + 128]).then_inc(T.sem["st%d" % n], 16)
        if n + PLANES < N:
            refill(scal, n + PLANES, "p")
    for n in range(N - STAGE, N):
        scal.wait_ge(T.sem["st%d" % n], 16)
    g.wait_ge(T.sem.sent, total)
